import numpy as np
import ml_dtypes


def mxq(x, axis, fmt="e4m3"):
    dtype, down = {"e4m3": (ml_dtypes.float8_e4m3fn, 7), "e5m2": (ml_dtypes.float8_e5m2, 14)}[fmt]
    v = np.moveaxis(np.asarray(x, np.float32).astype(ml_dtypes.bfloat16).astype(np.float64), axis, -1)
    blocks = v.reshape(v.shape[:-1] + (-1, 32))
    amax = np.abs(blocks).max(-1, keepdims=True)
    byte = np.maximum(np.where(amax > 0, np.frexp(amax)[1] - 1 + 127, 0) - down, 1)
    scale = np.exp2(byte - 127.0)
    codes = (blocks / scale).astype(np.float32).astype(dtype).astype(np.float64)
    return np.moveaxis((codes * scale).reshape(v.shape), -1, axis)


WIDE = False


def mx_kscale(k):
    if not WIDE:
        return np.ones(k)
    levels = np.array([10, -10, 5, -5, 0])
    if k % 512:
        return np.exp2(np.random.permutation(np.resize(levels, k // 32))).repeat(32)
    a = np.empty((k // 512, 16))
    for p in range(k // 512):
        a[p, :8] = np.random.permutation(np.resize(levels, 8))
        for g in range(8):
            far = levels[np.abs(levels - a[p, g]) >= 10]
            a[p, g + 8] = far[np.random.randint(len(far))]
    return np.exp2(a.ravel()).repeat(32)


BF16 = ml_dtypes.bfloat16


def bf(x):
    return np.asarray(x, np.float32).astype(BF16)


def f64(x):
    return np.asarray(x).astype(np.float64)


E2M1 = np.array([0.0, 0.5, 1.0, 1.5, 2.0, 3.0, 4.0, 6.0, -0.0, -0.5, -1.0, -1.5, -2.0, -3.0, -4.0, -6.0])


def pack_weight(w, fmt):
    k, n = w.shape
    w = f64(bf(w)).reshape(k // 32, 32, n)
    amax = np.abs(w).max(1)
    if fmt == "e4m3":
        byte = np.frexp(amax)[1] - 1 + 127 - 7
    else:
        mant, ex = np.frexp(amax / 6.0)
        byte = np.where(mant > 0.5, ex, ex - 1) + 127
    byte = np.clip(np.where(amax > 0, byte, 1), 1, 254)
    scaled = (w * np.exp2(127.0 - byte)[:, None, :]).reshape(k, n).astype(np.float32)
    by_word = np.ascontiguousarray(scaled.reshape(k // 512, 128, 4, n).transpose(0, 1, 3, 2))
    if fmt == "e4m3":
        words = by_word.astype(ml_dtypes.float8_e4m3fn).view(np.uint8)
    else:
        c = by_word.astype(ml_dtypes.float4_e2m1fn).view(np.uint8) & 0xF
        words = c[..., 0::2] | (c[..., 1::2] << 4)
    return np.ascontiguousarray(words), np.ascontiguousarray(byte.astype(np.uint8).reshape(k // 512, 16, n))


def unpack_weight(words, scales, fmt):
    g, p, n, _ = words.shape
    if fmt == "e4m3":
        vals = np.ascontiguousarray(words).view(ml_dtypes.float8_e4m3fn).astype(np.float64)
    else:
        nib = np.empty((g, p, n, 4), np.uint8)
        nib[..., 0::2] = words & 0xF
        nib[..., 1::2] = words >> 4
        vals = E2M1[nib]
    vals = vals * np.repeat(np.exp2(scales.astype(np.float64) - 127.0), 8, axis=1)[..., None]
    return vals.transpose(0, 1, 3, 2).reshape(g * 512, n)
def pack4(w):
    words, scales = pack_weight(w, "e2m1")
    return words.reshape(words.shape[0], 128, -1), scales


def unpack4(words, scales):
    return unpack_weight(words.reshape(words.shape[0], 128, -1, 2), scales, "e2m1")


E4M3FN = np.array([(-1.0 if i & 128 else 1.0) * ((1.0 + (i & 7) / 8.0) * 2.0 ** (((i >> 3) & 15) - 7) if i & 120 else (i & 7) * 2.0 ** -9) for i in range(256)])


def e4m3fn_bytes(y):
    return np.clip(np.asarray(y, np.float64), -448.0, 448.0).astype(np.float32).astype(ml_dtypes.float8_e4m3fn).view(np.uint8)


def e4m3fn_values(b):
    return E4M3FN[b]


B, D, F, K = 1024, 512, 1024, 2


def draw0():
    u, t = mx_kscale(D), mx_kscale(F)
    inputs = {
        "x": bf(np.random.standard_normal((B, D)) * u),
        "cs": bf(np.random.standard_normal((K, D, F)) / np.sqrt(D) / u[None, :, None]),
        "ss": bf(np.random.standard_normal((K, D, F)) / np.sqrt(D) / u[None, :, None]),
        "gamma": bf(np.random.uniform(0.5, 1.5, (K, F))),
        "g": bf((1.0 + 0.1 * np.random.standard_normal(F)) * t),
    }
    words, scales = pack4(np.random.standard_normal((F, D)) / np.sqrt(F) / t[:, None])
    inputs["dv_words"] = words
    inputs["dv_scales"] = scales
    return inputs


def weno_alpha(s, gamma_k):
    d = 0.5 + s * s
    return gamma_k / (d * d)


def burgers_flux(qh):
    return qh + 0.5 * qh * qh


def core(x, cs, ss, gamma, g, dv_words, dv_scales):
    cs, ss, gamma, g = f64(cs), f64(ss), f64(gamma), f64(g)
    xq = mxq(f64(x), 1, "e4m3")
    q = [(xq @ mxq(cs[k], 0, "e4m3")) for k in range(K)]
    s = [(xq @ mxq(ss[k], 0, "e4m3")) for k in range(K)]
    al = [weno_alpha(s[k], gamma[k][None, :]) for k in range(K)]
    qh = (al[0] * q[0] + al[1] * q[1]) / (al[0] + al[1])
    phi = burgers_flux(qh)
    pg = phi * g[None, :]
    return mxq(pg, 1, "e4m3") @ unpack4(dv_words, dv_scales)


def setup_inputs():
    drawn = draw0()
    full = np.asarray(drawn['ss']).astype(np.float64)
    scale = (np.abs(full).reshape(2, 512, 8, 128).max(axis=(3,)) / 448.0).astype(np.float32)
    given = {}
    for key, value in drawn.items():
        if key == 'ss':
            given['ss_bytes'] = e4m3fn_bytes(full / np.repeat(scale.astype(np.float64), 128, axis=2))
            given['ss_scale'] = scale
        else:
            given[key] = value
    return given


def reference(x, cs, ss_bytes, ss_scale, gamma, g, dv_words, dv_scales):
    return core(x, cs, e4m3fn_values(ss_bytes) * np.repeat(ss_scale.astype(np.float64), 128, axis=2), gamma, g, dv_words, dv_scales)

@@ -1,0 +1,354 @@
+from contextlib import ExitStack
+
+import concourse.mybir as mybir
+from concourse.masks import make_identity
+
+F32 = mybir.dt.float32
+BF16 = mybir.dt.bfloat16
+I32 = mybir.dt.int32
+U32 = mybir.dt.uint32
+U8 = mybir.dt.uint8
+FP8 = mybir.dt.float8_e4m3fn
+FP8X4 = mybir.dt.float8_e4m3fn_x4
+FP4X4 = mybir.dt.float4_e2m1fn_x4
+ALU = mybir.AluOpType
+ACT = mybir.ActivationFunctionType
+
+FLOPS = 2 * 5 * 1024 * 512 * 1024
+P = 128
+TILES = 8
+
+
+def tile_learnedstencilwenostep_d1p_kernel(
+    tc, x, cs, ss_bytes, ss_scale, gamma, g, dv_words, dv_scales, out
+):
+    nc = tc.nc
+    with ExitStack() as ctx:
+        ctx.enter_context(tc.manual_schedule())
+        keep = ctx.enter_context(tc.tile_pool(name="keep", bufs=1))
+        work = ctx.enter_context(tc.tile_pool(name="work", bufs=2))
+        flow = ctx.enter_context(tc.tile_pool(name="flow", bufs=6))
+        psum = ctx.enter_context(tc.psum_pool(name="psum", bufs=1))
+
+        xr = keep.tile([P, TILES, 512], BF16, name="xr")
+        xt = keep.tile([P, TILES, 128, 4], BF16, name="xt", align_bytes=64)
+        xn = keep.tile([P, TILES, 128, 4], BF16, name="xn", align_bytes=64)
+        xq = keep.tile([P, 2, 1024], U32, name="xq", align_bytes=64)
+        xs = keep.tile([P, 2, 1024], U8, name="xs", align_bytes=64)
+        sb = keep.tile([P, 2, 4, 1024], U8, name="sb", align_bytes=64)
+        scl = keep.tile([P, 2, 32], F32, name="scl")
+        ssq = keep.tile([P, 2, 2, 512], U32, name="ssq", align_bytes=64)
+        sss = keep.tile([P, 2, 2, 512], U8, name="sss", align_bytes=64)
+        cb = keep.tile([P, 2, 4, 1024], BF16, name="cb", align_bytes=64)
+        csq = keep.tile([P, 2, 2, 512], U32, name="csq", align_bytes=64)
+        css = keep.tile([P, 2, 2, 512], U8, name="css", align_bytes=64)
+        lg = keep.tile([P, 2, 2, 4, 1024], F32, name="lg")
+        pg = keep.tile([P, TILES, 1024], BF16, name="pg", align_bytes=64)
+        dvw = keep.tile([P, 2, 1024], U8, name="dvw", align_bytes=64)
+        dvs = keep.tile([P, 2, 512], U8, name="dvs", align_bytes=64)
+        gmb = keep.tile([P, 2, 2, 4], BF16, name="gmb")
+        gb = keep.tile([P, 2, 4], BF16, name="gb")
+        gmf = keep.tile([P, 16], F32, name="gmf")
+        half = keep.tile([P, 16], F32, name="half")
+        rt = keep.tile([P, 16], F32, name="rt")
+        rth = keep.tile([P, 16], F32, name="rth")
+        gh = keep.tile([P, 2, 4], F32, name="gh")
+        ident = keep.tile([P, P], F32, name="ident")
+        warm = keep.tile([P, 1], F32, name="warm")
+
+        xv = x.rearrange("(p i) d -> p i d", i=TILES)
+        ov = out.rearrange("(p i) d -> p i d", i=TILES)
+
+        sv = [ss_bytes[k].rearrange("(p t) n -> p t n", t=4) for k in range(2)]
+        nc.scalar.dma_start(out=scl[:], in_=ss_scale.rearrange("k (p t) j -> p k (t j)", t=4))
+        nc.sync.dma_start(out=sb[:, 0, :, 0:512], in_=sv[0][:, :, 0:512])
+        nc.sync.dma_start(out=xr[:, 0:4, :], in_=xv[:, 0:4, :])
+        nc.sync.dma_start(out=sb[:, 1, :, 0:512], in_=sv[1][:, :, 0:512])
+        nc.sync.dma_start(out=xr[:, 4:8, :], in_=xv[:, 4:8, :])
+        nc.scalar.dma_start(out=gmb[:].rearrange("p k u t -> p (k u) t"), in_=gamma.rearrange("k (u p t) -> p (k u) t", p=P, t=4))
+        nc.scalar.dma_start(out=gb[:], in_=g.rearrange("(u p t) -> p u t", p=P, t=4))
+        for k in range(2):
+            nc.sync.dma_start(out=sb[:, k, :, 512:1024], in_=sv[k][:, :, 512:1024])
+        for k in range(2):
+            nc.sync.dma_start(out=cb[:, k, :, :], in_=cs[k].rearrange("(p t) n -> p t n", t=4))
+        nc.sync.dma_start(out=dvw[:].bitcast(I32), in_=dv_words.rearrange("g p n -> p g n").bitcast(I32))
+
+        nc.vector.memset(warm[:], 1.0)
+        nc.scalar.activation(out=warm[:], in_=warm[:], func=ACT.Ln)
+        make_identity(nc, ident[:])
+        nc.vector.memset(dvs[:].rearrange("p g n -> p (g n)").bitcast(I32), 0)
+        for q in range(4):
+            nc.sync.dma_start(
+                out=dvs[32 * q : 32 * q + 4, :, :].bitcast(I32),
+                in_=dv_scales[:, 4 * q : 4 * q + 4, :].rearrange("g r n -> r g n").bitcast(I32),
+            )
+        nc.gpsimd.memset(half[:], 0.5)
+        nc.gpsimd.tensor_scalar(out=gmf[:], in0=gmb[:].rearrange("p k u t -> p (k u t)"), scalar1=1e-30, scalar2=None, op0=ALU.max)
+        nc.gpsimd.tensor_tensor(out=rt[:], in0=gmf[:], in1=half[:], op=ALU.pow)
+        nc.gpsimd.tensor_scalar(out=rth[:], in0=rt[:], scalar1=0.5, scalar2=None, op0=ALU.mult)
+        nc.gpsimd.tensor_scalar(out=gh[:].rearrange("p u t -> p (u t)"), in0=gb[:].rearrange("p u t -> p (u t)"), scalar1=0.5, scalar2=None, op0=ALU.mult)
+
+        words = xr[:].rearrange("p i d -> p (i d)").bitcast(F32)
+
+        def turn_x(pair, eng):
+            bank = psum.tile([P, 2, 2, 128], F32, tag="dq"[pair % 2], name="xbank", bufs=2)
+            for ii in range(2):
+                i = 2 * pair + ii
+                for u in range(2):
+                    nc.tensor.transpose(bank[:, ii, u, :], words[:, 256 * i + u : 256 * (i + 1) : 2], ident[:])
+            dst = xt[:, 2 * pair : 2 * pair + 2, :, :].rearrange("p i r t -> p (i r t)").bitcast(F32).rearrange("p (i r u) -> p i r u", i=2, u=2)
+            src = bank[:].rearrange("p i u r -> p i r u")
+            if eng == "S":
+                nc.scalar.copy(out=dst, in_=src)
+            else:
+                nc.vector.tensor_copy(out=dst, in_=src)
+
+        def quant_x(sign, t0, t1):
+            src = (xt if sign == 0 else xn)[:, t0:t1, :, :].rearrange("p i r t -> p (i r t)")
+            nc.vector.quantize_mx(out=xq[:, sign, 128 * t0 : 128 * t1].bitcast(FP8X4), scales=xs[:, sign, 128 * t0 : 128 * t1], in_=src)
+
+        def negate_x(t0, t1):
+            nc.vector.tensor_scalar(
+                out=xn[:, t0:t1, :, :].rearrange("p i r t -> p (i r t)"),
+                in0=xt[:, t0:t1, :, :].rearrange("p i r t -> p (i r t)"),
+                scalar1=-1.0, scalar2=None, op0=ALU.mult)
+
+        st = {}
+        wide = {}
+        grouped = {}
+
+        def widen(k, u, eng, ts=range(4)):
+            if (k, u) not in wide:
+                wide[k, u] = work.tile([P, 4, 512], BF16, name="wide", tag="wide", bufs=3)
+            for t in ts:
+                for j in range(4):
+                    dst = wide[k, u][:, t, 128 * j : 128 * j + 128]
+                    src = sb[:, k, t, 512 * u + 128 * j : 512 * u + 128 * j + 128].bitcast(FP8)
+                    col = 8 * t + 4 * u + j
+                    if eng == "S":
+                        nc.scalar.activation(out=dst, in_=src, func=ACT.Copy, scale=scl[:, k, col : col + 1])
+                    else:
+                        nc.vector.tensor_scalar(out=dst, in0=src, scalar1=scl[:, k, col : col + 1], scalar2=None, op0=ALU.mult)
+
+        def weave_in(key, src, halves=(0, 1)):
+            if key not in grouped:
+                grouped[key] = work.tile([P, 2048], BF16, name="grouped", tag="grouped", bufs=4, align_bytes=64)
+            h0, h1 = halves[0], halves[-1] + 1
+            nc.vector.tensor_copy(
+                out=grouped[key][:, 1024 * h0 : 1024 * h1].rearrange("p (tf m j) -> p tf m j", m=128, j=4),
+                in_=src.rearrange("p j (m tf) -> p tf m j", tf=4)[:, 2 * h0 : 2 * h1])
+
+        def ss_il(k, u, halves=(0, 1)):
+            weave_in(("s", k, u), wide[k, u][:], halves)
+
+        def ss_q(k, u, halves=(0, 1)):
+            h0, h1 = halves[0], halves[-1] + 1
+            nc.vector.quantize_mx(out=ssq[:, k, u, 256 * h0 : 256 * h1].bitcast(FP8X4), scales=sss[:, k, u, 256 * h0 : 256 * h1], in_=grouped["s", k, u][:, 1024 * h0 : 1024 * h1])
+
+        def cs_il(k, u):
+            weave_in(("c", k, u), cb[:, k, :, 512 * u : 512 * u + 512])
+
+        def cs_q(k, u):
+            nc.vector.quantize_mx(out=csq[:, k, u, :].bitcast(FP8X4), scales=css[:, k, u, :], in_=grouped["c", k, u][:])
+
+        def mm(dst, w, wsc, k, u, t, sign, c0, c1, start, stop):
+            nc.tensor.matmul_mx(
+                out=dst, lhsT=w[:, k, u, 128 * t : 128 * t + 128].bitcast(FP8X4), lhsT_scale=wsc[:, k, u, 128 * t : 128 * t + 128],
+                rhs=xq[:, sign, c0:c1].bitcast(FP8X4), rhs_scale=xs[:, sign, c0:c1], start=start, stop=stop)
+
+        def a_sq(u, t, k, h, eng="S"):
+            c0, c1 = 512 * h, 512 * h + 512
+            ps = psum.tile([P, 512], F32, name="sbank", tag="s", bufs=4)
+            mm(ps[:], ssq, sss, k, u, t, 0, c0, c1, True, True)
+            dst = lg[:, k, u, t, c0:c1]
+            if eng == "S":
+                nc.scalar.activation(out=dst, in_=ps[:], func=ACT.Square)
+            else:
+                nc.vector.tensor_copy(out=dst, in_=ps[:])
+
+        def a_mul(u, t, k, h):
+            dst = lg[:, k, u, t, 512 * h : 512 * h + 512]
+            nc.vector.tensor_tensor(out=dst, in0=dst, in1=dst, op=ALU.mult)
+
+        def a_ln(u, t, k):
+            j = 8 * (1 - k) + 4 * u + t
+            v = lg[:, k, u, t, :]
+            nc.scalar.activation(out=v, in_=v, func=ACT.Ln, bias=rth[:, j : j + 1], scale=rt[:, j : j + 1])
+
+        def a_sub(u, t, eng):
+            e = nc.vector if eng == "V" else nc.gpsimd
+            e.tensor_tensor(out=lg[:, 0, u, t, :], in0=lg[:, 0, u, t, :], in1=lg[:, 1, u, t, :], op=ALU.subtract)
+
+        def sig(i, u):
+            st["w", i, u] = flow.tile([P, 512], F32, name="w", tag="w", bufs=8)
+            nc.scalar.activation(
+                out=bt(st["w", i, u][:]),
+                in_=lg[:, 0, u, :, 128 * i : 128 * i + 128].rearrange("p t b -> p b t"),
+                func=ACT.Sigmoid, scale=2.0)
+
+        def b_mm(i, u):
+            qb = psum.tile([P, 4, 128], F32, name="qbank", tag="q", bufs=2)
+            db = psum.tile([P, 4, 128], F32, name="dbank", tag="d", bufs=2)
+            c0, c1 = 128 * i, 128 * i + 128
+            for t in range(4):
+                mm(db[:, t, :], csq, css, 1, u, t, 0, c0, c1, True, False)
+                mm(db[:, t, :], csq, css, 0, u, t, 1, c0, c1, False, True)
+            for t in range(4):
+                mm(qb[:, t, :], csq, css, 0, u, t, 0, c0, c1, True, True)
+            st["q", i, u], st["d", i, u] = qb, db
+
+        def bt(ap):
+            return ap.rearrange("p (b t) -> p b t", t=4)
+
+        def b_td(i, u):
+            v = flow.tile([P, 512], F32, name="v", tag="v", bufs=5)
+            nc.vector.tensor_tensor(out=bt(v[:]), in0=st["d", i, u][:].rearrange("p t b -> p b t"), in1=bt(st["w", i, u][:]), op=ALU.mult)
+            st["v", i, u] = v
+
+        def b_qh(i, u):
+            v = st["v", i, u]
+            nc.vector.tensor_tensor(out=bt(v[:]), in0=st["q", i, u][:].rearrange("p t b -> p b t"), in1=bt(v[:]), op=ALU.add)
+
+        def b_flux(i, u, eng):
+            v = st["v", i, u]
+            if eng == "S":
+                nc.scalar.activation(out=v[:], in_=v[:], func=ACT.Square, bias=1.0)
+            else:
+                nc.vector.scalar_tensor_tensor(out=v[:], in0=v[:], scalar=2.0, in1=v[:], op0=ALU.add, op1=ALU.mult)
+
+        def b_fin(i, u, eng):
+            v = st["v", i, u]
+            dst = bt(pg[:, i, 512 * u : 512 * u + 512])
+            gbc = gh[:, u, :].unsqueeze(1).to_broadcast([P, 128, 4])
+            if eng == "S":
+                nc.vector.scalar_tensor_tensor(out=dst, in0=bt(v[:]), scalar=-1.0, in1=gbc, op0=ALU.add, op1=ALU.mult)
+            else:
+                nc.vector.tensor_tensor(out=dst, in0=bt(v[:]), in1=gbc, op=ALU.mult)
+
+        def b_quant(i):
+            cq = flow.tile([P, 256], U32, name="cq", tag="cq", bufs=3, align_bytes=64)
+            sq = flow.tile([P, 256], U8, name="sq", tag="sq", bufs=3, align_bytes=64)
+            nc.vector.quantize_mx(out=cq[:].bitcast(FP8X4), scales=sq[:], in_=pg[:, i, :])
+            st["c", i] = (cq, sq)
+
+        def b_out(i):
+            cq, sq = st["c", i]
+            ob = psum.tile([P, 512], F32, name="obank", tag="s", bufs=4)
+            for u in range(2):
+                nc.tensor.matmul_mx(
+                    out=ob[:], lhsT=cq[:, 128 * u : 128 * u + 128].bitcast(FP8X4), lhsT_scale=sq[:, 128 * u : 128 * u + 128],
+                    rhs=dvw[:, u, :].bitcast(FP4X4), rhs_scale=dvs[:, u, :], start=(u == 0), stop=(u == 1))
+            st["o", i] = ob
+
+        def b_evac(i, eng):
+            ob = st["o", i]
+            ot = flow.tile([P, 512], F32, name="ot", tag="ot", bufs=4)
+            if eng == "S":
+                nc.scalar.copy(out=ot[:], in_=ob[:])
+            else:
+                nc.vector.tensor_copy(out=ot[:], in_=ob[:])
+            nc.sync.dma_start(out=ov[:, i, :], in_=ot[:])
+
+
+        FLUX0 = "VVVVVVVV"
+        FLUX1 = "SSSSSSSS"
+        SUB1 = "VVVV"
+        EVAC = "SSSSSSSS"
+        widen(0, 0, "S", (0, 1))
+        widen(0, 0, "V", (2, 3))
+        turn_x(0, "S")
+        ss_il(0, 0, (0,))
+        turn_x(1, "S")
+        ss_q(0, 0, (0,))
+        ss_il(0, 0, (1,))
+        quant_x(0, 0, 4)
+        ss_q(0, 0, (1,))
+        for t in range(4):
+            widen(1, 0, "SSSS"[t], (t,))
+        for t in range(2):
+            a_sq(0, t, 0, 0)
+        ss_il(1, 0)
+        turn_x(2, "S")
+        turn_x(3, "S")
+        for t in range(2, 4):
+            a_sq(0, t, 0, 0)
+        ss_q(1, 0)
+        quant_x(0, 4, 8)
+        for t in range(4):
+            a_sq(0, t, 1, 0)
+        for t in range(4):
+            a_sq(0, t, 0, 1)
+            a_sq(0, t, 1, 1)
+        for t in range(4):
+            for k in range(2):
+                a_ln(0, t, k)
+        negate_x(0, 4)
+        cs_il(0, 0)
+        quant_x(1, 0, 4)
+        cs_il(1, 0)
+        cs_q(0, 0)
+        widen(0, 1, "V")
+        cs_q(1, 0)
+        ss_il(0, 1)
+        widen(1, 1, "V")
+        ss_q(0, 1)
+        ss_il(1, 1)
+        negate_x(4, 8)
+        ss_q(1, 1)
+        quant_x(1, 4, 8)
+        for t in range(4):
+            a_sub(0, t, "V")
+        for i in range(8):
+            sig(i, 0)
+        b_mm(0, 0)
+        extra = [
+            lambda: cs_il(0, 1),
+            lambda: cs_il(1, 1),
+            lambda: cs_q(0, 1),
+            lambda: cs_q(1, 1),
+        ]
+        for m in range(TILES + 4):
+            n = m - 2
+            if 0 <= n < TILES:
+                for h in range(2):
+                    a_sq(1, n // 2, n % 2, h)
+            if 1 <= n < TILES + 1:
+                a_ln(1, (n - 1) // 2, (n - 1) % 2)
+            if m < TILES:
+                b_td(m, 0)
+            if 0 <= m - 1 < TILES:
+                b_qh(m - 1, 0)
+            if m + 1 < TILES:
+                b_mm(m + 1, 0)
+            if 0 <= m - 2 < TILES:
+                b_flux(m - 2, 0, FLUX0[m - 2])
+            if 0 <= m - 3 < TILES:
+                b_fin(m - 3, 0, FLUX0[m - 3])
+            if 3 <= m < 3 + 4:
+                extra[m - 3]()
+            if m >= 6 and m % 2 == 6 % 2 and (m - 6) // 2 < 3:
+                a_sub(1, (m - 6) // 2, SUB1[(m - 6) // 2])
+        for t in range(4):
+            if 2 * t + 6 >= TILES + 4 or t == 3:
+                a_sub(1, t, SUB1[t])
+        sig(0, 1)
+        sig(1, 1)
+        b_mm(0, 1)
+        for m in range(TILES + 6):
+            if m < TILES:
+                b_td(m, 1)
+            if 0 <= m - 1 < TILES:
+                b_qh(m - 1, 1)
+            if m + 1 < TILES:
+                b_mm(m + 1, 1)
+            if 0 <= m - 2 < TILES:
+                b_flux(m - 2, 1, FLUX1[m - 2])
+            if m + 2 < TILES:
+                sig(m + 2, 1)
+            if 0 <= m - 3 < TILES:
+                b_fin(m - 3, 1, FLUX1[m - 3])
+            if 0 <= m - 4 < TILES:
+                b_quant(m - 4)
+                b_out(m - 4)
+            if 0 <= m - 6 + 1 < TILES:
+                b_evac(m - 6 + 1, EVAC[m - 6 + 1])

@@ -27,7 +27,6 @@ def tile_learnedstencilwenostep_d1p_kernel(
         ctx.enter_context(tc.manual_schedule())
         keep = ctx.enter_context(tc.tile_pool(name="keep", bufs=1))
         work = ctx.enter_context(tc.tile_pool(name="work", bufs=2))
-        flow = ctx.enter_context(tc.tile_pool(name="flow", bufs=6))
         psum = ctx.enter_context(tc.psum_pool(name="psum", bufs=1))
 
         xr = keep.tile([P, TILES, 512], BF16, name="xr")
@@ -43,7 +42,10 @@ def tile_learnedstencilwenostep_d1p_kernel(
         csq = keep.tile([P, 2, 2, 512], U32, name="csq", align_bytes=64)
         css = keep.tile([P, 2, 2, 512], U8, name="css", align_bytes=64)
         lg = keep.tile([P, 2, 2, 4, 1024], F32, name="lg")
-        pg = keep.tile([P, TILES, 1024], BF16, name="pg", align_bytes=64)
+        pg = keep.tile([P, 2, 4096], BF16, name="pg", align_bytes=64)
+        pq = keep.tile([P, 2, 1024], U32, name="pq", align_bytes=64)
+        ps8 = keep.tile([P, 2, 1024], U8, name="ps8", align_bytes=64)
+        ghn = keep.tile([P, 2, 4], F32, name="ghn")
         dvw = keep.tile([P, 2, 1024], U8, name="dvw", align_bytes=64)
         dvs = keep.tile([P, 2, 512], U8, name="dvs", align_bytes=64)
         gmb = keep.tile([P, 2, 2, 4], BF16, name="gmb")
@@ -87,6 +89,7 @@ def tile_learnedstencilwenostep_d1p_kernel(
         nc.gpsimd.tensor_tensor(out=rt[:], in0=gmf[:], in1=half[:], op=ALU.pow)
         nc.gpsimd.tensor_scalar(out=rth[:], in0=rt[:], scalar1=0.5, scalar2=None, op0=ALU.mult)
         nc.gpsimd.tensor_scalar(out=gh[:].rearrange("p u t -> p (u t)"), in0=gb[:].rearrange("p u t -> p (u t)"), scalar1=0.5, scalar2=None, op0=ALU.mult)
+        nc.gpsimd.tensor_scalar(out=ghn[:].rearrange("p u t -> p (u t)"), in0=gb[:].rearrange("p u t -> p (u t)"), scalar1=-0.5, scalar2=None, op0=ALU.mult)
 
         words = xr[:].rearrange("p i d -> p (i d)").bitcast(F32)
 
@@ -135,8 +138,8 @@ def tile_learnedstencilwenostep_d1p_kernel(
                 grouped[key] = work.tile([P, 2048], BF16, name="grouped", tag="grouped", bufs=4, align_bytes=64)
             h0, h1 = halves[0], halves[-1] + 1
             nc.vector.tensor_copy(
-                out=grouped[key][:, 1024 * h0 : 1024 * h1].rearrange("p (tf m j) -> p tf m j", m=128, j=4),
-                in_=src.rearrange("p j (m tf) -> p tf m j", tf=4)[:, 2 * h0 : 2 * h1])
+                out=grouped[key][:, 1024 * h0 : 1024 * h1].rearrange("p (tf m j) -> p m j tf", m=128, j=4),
+                in_=src.rearrange("p j (m tf) -> p m j tf", tf=4)[:, :, :, 2 * h0 : 2 * h1])
 
         def ss_il(k, u, halves=(0, 1)):
             weave_in(("s", k, u), wide[k, u][:], halves)
@@ -179,74 +182,90 @@ def tile_learnedstencilwenostep_d1p_kernel(
             e = nc.vector if eng == "V" else nc.gpsimd
             e.tensor_tensor(out=lg[:, 0, u, t, :], in0=lg[:, 0, u, t, :], in1=lg[:, 1, u, t, :], op=ALU.subtract)
 
-        def sig(i, u):
-            st["w", i, u] = flow.tile([P, 512], F32, name="w", tag="w", bufs=8)
-            nc.scalar.activation(
-                out=bt(st["w", i, u][:]),
-                in_=lg[:, 0, u, :, 128 * i : 128 * i + 128].rearrange("p t b -> p b t"),
-                func=ACT.Sigmoid, scale=2.0)
+        def zone(unit):
+            if unit[0] == "t":
+                return lg[:, 0, unit[1], unit[2], 512 * unit[3] : 512 * unit[3] + 512]
+            return lg[:, 0, unit[1], :, 128 * unit[2] : 128 * unit[2] + 128]
 
-        def b_mm(i, u):
-            qb = psum.tile([P, 4, 128], F32, name="qbank", tag="q", bufs=2)
-            db = psum.tile([P, 4, 128], F32, name="dbank", tag="d", bufs=2)
-            c0, c1 = 128 * i, 128 * i + 128
-            for t in range(4):
-                mm(db[:, t, :], csq, css, 1, u, t, 0, c0, c1, True, False)
-                mm(db[:, t, :], csq, css, 0, u, t, 1, c0, c1, False, True)
-            for t in range(4):
-                mm(qb[:, t, :], csq, css, 0, u, t, 0, c0, c1, True, True)
-            st["q", i, u], st["d", i, u] = qb, db
+        def like(unit, ap):
+            return ap if unit[0] == "t" else ap.rearrange("p (t b) -> p t b", t=4)
 
-        def bt(ap):
-            return ap.rearrange("p (b t) -> p b t", t=4)
+        def sig(unit):
+            nc.scalar.activation(out=zone(unit), in_=zone(unit), func=ACT.Sigmoid, scale=2.0)
 
-        def b_td(i, u):
-            v = flow.tile([P, 512], F32, name="v", tag="v", bufs=5)
-            nc.vector.tensor_tensor(out=bt(v[:]), in0=st["d", i, u][:].rearrange("p t b -> p b t"), in1=bt(st["w", i, u][:]), op=ALU.mult)
-            st["v", i, u] = v
-
-        def b_qh(i, u):
-            v = st["v", i, u]
-            nc.vector.tensor_tensor(out=bt(v[:]), in0=st["q", i, u][:].rearrange("p t b -> p b t"), in1=bt(v[:]), op=ALU.add)
-
-        def b_flux(i, u, eng):
-            v = st["v", i, u]
-            if eng == "S":
-                nc.scalar.activation(out=v[:], in_=v[:], func=ACT.Square, bias=1.0)
+        def b_mm(unit):
+            u = unit[1]
+            qb = psum.tile([P, 512], F32, name="qbank", tag="q", bufs=2)
+            db = psum.tile([P, 512], F32, name="dbank", tag="d", bufs=2)
+            if unit[0] == "t":
+                jobs = [(unit[2], 0, 512, 512 * unit[3])]
             else:
-                nc.vector.scalar_tensor_tensor(out=v[:], in0=v[:], scalar=2.0, in1=v[:], op0=ALU.add, op1=ALU.mult)
+                jobs = [(t, 128 * t, 128, 128 * unit[2]) for t in range(4)]
+            for t, o, n, c0 in jobs:
+                mm(db[:, o : o + n], csq, css, 1, u, t, 0, c0, c0 + n, True, False)
+                mm(db[:, o : o + n], csq, css, 0, u, t, 1, c0, c0 + n, False, True)
+            for t, o, n, c0 in jobs:
+                mm(qb[:, o : o + n], csq, css, 0, u, t, 0, c0, c0 + n, True, True)
+            st["q", unit], st["d", unit] = qb, db
 
-        def b_fin(i, u, eng):
-            v = st["v", i, u]
-            dst = bt(pg[:, i, 512 * u : 512 * u + 512])
-            gbc = gh[:, u, :].unsqueeze(1).to_broadcast([P, 128, 4])
+        def b_td(unit):
+            nc.vector.tensor_tensor(out=zone(unit), in0=like(unit, st["d", unit][:]), in1=zone(unit), op=ALU.mult)
+
+        def b_qh(unit):
+            nc.vector.tensor_tensor(out=zone(unit), in0=like(unit, st["q", unit][:]), in1=zone(unit), op=ALU.add)
+
+        def b_flux(unit, eng):
+            v = zone(unit)
             if eng == "S":
-                nc.vector.scalar_tensor_tensor(out=dst, in0=bt(v[:]), scalar=-1.0, in1=gbc, op0=ALU.add, op1=ALU.mult)
+                nc.scalar.activation(out=v, in_=v, func=ACT.Square, bias=1.0)
             else:
-                nc.vector.tensor_tensor(out=dst, in0=bt(v[:]), in1=gbc, op=ALU.mult)
+                nc.vector.scalar_tensor_tensor(out=v, in0=v, scalar=2.0, in1=v, op0=ALU.add, op1=ALU.mult)
 
-        def b_quant(i):
-            cq = flow.tile([P, 256], U32, name="cq", tag="cq", bufs=3, align_bytes=64)
-            sq = flow.tile([P, 256], U8, name="sq", tag="sq", bufs=3, align_bytes=64)
-            nc.vector.quantize_mx(out=cq[:].bitcast(FP8X4), scales=sq[:], in_=pg[:, i, :])
-            st["c", i] = (cq, sq)
+        def b_fin(unit, eng):
+            u = unit[1]
+            if unit[0] == "t":
+                if unit[2] == 0:
+                    st["pt", u, unit[3]] = work.tile([P, 4, 512], BF16, name="pgt", tag="pgt", bufs=2)
+                jobs = [(unit[2], st["pt", u, unit[3]][:, unit[2], :], zone(unit))]
+            else:
+                st["pi", unit[2]] = work.tile([P, 4, 128], BF16, name="pgi", tag="pgi", bufs=2)
+                jobs = [(t, st["pi", unit[2]][:, t, :], zone(unit)[:, t, :]) for t in range(4)]
+            for t, dst, src in jobs:
+                if eng == "S":
+                    nc.vector.tensor_scalar(out=dst, in0=src, scalar1=gh[:, u, t : t + 1], scalar2=ghn[:, u, t : t + 1], op0=ALU.mult, op1=ALU.add)
+                else:
+                    nc.vector.tensor_scalar(out=dst, in0=src, scalar1=gh[:, u, t : t + 1], scalar2=None, op0=ALU.mult)
+
+        def span(unit):
+            return (512 * unit[3], 512) if unit[0] == "t" else (128 * unit[2], 128)
+
+        def b_il(unit):
+            u = unit[1]
+            c0, n = span(unit)
+            src = st["pt", u, unit[3]] if unit[0] == "t" else st["pi", unit[2]]
+            nc.vector.tensor_copy(
+                out=pg[:, u, 4 * c0 : 4 * (c0 + n)].rearrange("p (c i t) -> p c t i", i=4, t=4),
+                in_=src[:].rearrange("p t (c i) -> p c t i", i=4))
+
+        def b_quant(unit):
+            u = unit[1]
+            c0, n = span(unit)
+            nc.vector.quantize_mx(out=pq[:, u, c0 : c0 + n].bitcast(FP8X4), scales=ps8[:, u, c0 : c0 + n], in_=pg[:, u, 4 * c0 : 4 * (c0 + n)])
 
         def b_out(i):
-            cq, sq = st["c", i]
             ob = psum.tile([P, 512], F32, name="obank", tag="s", bufs=4)
             for u in range(2):
                 nc.tensor.matmul_mx(
-                    out=ob[:], lhsT=cq[:, 128 * u : 128 * u + 128].bitcast(FP8X4), lhsT_scale=sq[:, 128 * u : 128 * u + 128],
+                    out=ob[:], lhsT=pq[:, u, 128 * i : 128 * i + 128].bitcast(FP8X4), lhsT_scale=ps8[:, u, 128 * i : 128 * i + 128],
                     rhs=dvw[:, u, :].bitcast(FP4X4), rhs_scale=dvs[:, u, :], start=(u == 0), stop=(u == 1))
             st["o", i] = ob
 
         def b_evac(i, eng):
-            ob = st["o", i]
-            ot = flow.tile([P, 512], F32, name="ot", tag="ot", bufs=4)
+            ot = work.tile([P, 512], F32, name="ot", tag="ot", bufs=4)
             if eng == "S":
-                nc.scalar.copy(out=ot[:], in_=ob[:])
+                nc.scalar.copy(out=ot[:], in_=st["o", i][:])
             else:
-                nc.vector.tensor_copy(out=ot[:], in_=ob[:])
+                nc.vector.tensor_copy(out=ot[:], in_=st["o", i][:])
             nc.sync.dma_start(out=ov[:, i, :], in_=ot[:])
 
 
@@ -298,9 +317,12 @@ def tile_learnedstencilwenostep_d1p_kernel(
         quant_x(1, 4, 8)
         for t in range(4):
             a_sub(0, t, "V")
-        for i in range(8):
-            sig(i, 0)
-        b_mm(0, 0)
+
+        units0 = [("t", 0, t, h) for h in range(2) for t in range(4)]
+        units1 = [("t", 1, t, 0) for t in range(4)] + [("i", 1, i) for i in range(4, 8)]
+        for unit in units0:
+            sig(unit)
+        b_mm(units0[0])
         extra = [
             lambda: cs_il(0, 1),
             lambda: cs_il(1, 1),
@@ -315,40 +337,59 @@ def tile_learnedstencilwenostep_d1p_kernel(
             if 1 <= n < TILES + 1:
                 a_ln(1, (n - 1) // 2, (n - 1) % 2)
             if m < TILES:
-                b_td(m, 0)
+                b_td(units0[m])
             if 0 <= m - 1 < TILES:
-                b_qh(m - 1, 0)
+                b_qh(units0[m - 1])
             if m + 1 < TILES:
-                b_mm(m + 1, 0)
+                b_mm(units0[m + 1])
             if 0 <= m - 2 < TILES:
-                b_flux(m - 2, 0, FLUX0[m - 2])
+                b_flux(units0[m - 2], FLUX0[m - 2])
             if 0 <= m - 3 < TILES:
-                b_fin(m - 3, 0, FLUX0[m - 3])
+                b_fin(units0[m - 3], FLUX0[m - 3])
             if 3 <= m < 3 + 4:
                 extra[m - 3]()
+            if m in (7, 11):
+                b_il(units0[m - 4])
+            if m == 8:
+                b_quant(units0[3])
             if m >= 6 and m % 2 == 6 % 2 and (m - 6) // 2 < 3:
                 a_sub(1, (m - 6) // 2, SUB1[(m - 6) // 2])
         for t in range(4):
             if 2 * t + 6 >= TILES + 4 or t == 3:
                 a_sub(1, t, SUB1[t])
-        sig(0, 1)
-        sig(1, 1)
-        b_mm(0, 1)
-        for m in range(TILES + 6):
+        sig(units1[0])
+        sig(units1[1])
+        b_mm(units1[0])
+        b_quant(units0[7])
+        EVACS = "SSSSSSSS"
+        outs = []
+        for m in range(TILES + 5):
             if m < TILES:
-                b_td(m, 1)
+                b_td(units1[m])
             if 0 <= m - 1 < TILES:
-                b_qh(m - 1, 1)
+                b_qh(units1[m - 1])
             if m + 1 < TILES:
-                b_mm(m + 1, 1)
+                b_mm(units1[m + 1])
             if 0 <= m - 2 < TILES:
-                b_flux(m - 2, 1, FLUX1[m - 2])
+                b_flux(units1[m - 2], FLUX1[m - 2])
             if m + 2 < TILES:
-                sig(m + 2, 1)
+                sig(units1[m + 2])
+            for _ in range(2):
+                if outs and outs[0][0] < m:
+                    i = outs.pop(0)[1]
+                    b_evac(i, EVACS[i])
+            if m >= 7 and m - 4 < TILES:
+                b_il(units1[m - 4])
             if 0 <= m - 3 < TILES:
-                b_fin(m - 3, 1, FLUX1[m - 3])
-            if 0 <= m - 4 < TILES:
-                b_quant(m - 4)
+                b_fin(units1[m - 3], FLUX1[m - 3])
+            if m == 7:
+                b_quant(units1[3])
+                outs += [(m, i) for i in range(4)]
+                for i in range(4):
+                    b_out(i)
+            if 8 <= m and m - 4 < TILES:
+                b_quant(units1[m - 4])
                 b_out(m - 4)
-            if 0 <= m - 6 + 1 < TILES:
-                b_evac(m - 6 + 1, EVAC[m - 6 + 1])
+                outs.append((m, m - 4))
+        for m, i in outs:
+            b_evac(i, EVACS[i])

@@ -31,9 +31,8 @@ def tile_learnedstencilwenostep_d1p_kernel(
 
         xr = keep.tile([P, TILES, 512], BF16, name="xr")
         xt = keep.tile([P, TILES, 128, 4], BF16, name="xt", align_bytes=64)
-        xn = keep.tile([P, TILES, 128, 4], BF16, name="xn", align_bytes=64)
-        xq = keep.tile([P, 2, 1024], U32, name="xq", align_bytes=64)
-        xs = keep.tile([P, 2, 1024], U8, name="xs", align_bytes=64)
+        xq = keep.tile([P, 1024], U32, name="xq", align_bytes=64)
+        xs = keep.tile([P, 1024], U8, name="xs", align_bytes=64)
         sb = keep.tile([P, 2, 4, 1024], U8, name="sb", align_bytes=64)
         scl = keep.tile([P, 2, 32], F32, name="scl")
         ssq = keep.tile([P, 2, 2, 512], U32, name="ssq", align_bytes=64)
@@ -106,15 +105,9 @@ def tile_learnedstencilwenostep_d1p_kernel(
             else:
                 nc.vector.tensor_copy(out=dst, in_=src)
 
-        def quant_x(sign, t0, t1):
-            src = (xt if sign == 0 else xn)[:, t0:t1, :, :].rearrange("p i r t -> p (i r t)")
-            nc.vector.quantize_mx(out=xq[:, sign, 128 * t0 : 128 * t1].bitcast(FP8X4), scales=xs[:, sign, 128 * t0 : 128 * t1], in_=src)
-
-        def negate_x(t0, t1):
-            nc.vector.tensor_scalar(
-                out=xn[:, t0:t1, :, :].rearrange("p i r t -> p (i r t)"),
-                in0=xt[:, t0:t1, :, :].rearrange("p i r t -> p (i r t)"),
-                scalar1=-1.0, scalar2=None, op0=ALU.mult)
+        def quant_x(t0, t1):
+            src = xt[:, t0:t1, :, :].rearrange("p i r t -> p (i r t)")
+            nc.vector.quantize_mx(out=xq[:, 128 * t0 : 128 * t1].bitcast(FP8X4), scales=xs[:, 128 * t0 : 128 * t1], in_=src)
 
         st = {}
         wide = {}
@@ -133,13 +126,16 @@ def tile_learnedstencilwenostep_d1p_kernel(
                     else:
                         nc.vector.tensor_scalar(out=dst, in0=src, scalar1=scl[:, k, col : col + 1], scalar2=None, op0=ALU.mult)
 
-        def weave_in(key, src, halves=(0, 1)):
+        def weave_in(key, src, halves=(0, 1), negate=False):
             if key not in grouped:
                 grouped[key] = work.tile([P, 2048], BF16, name="grouped", tag="grouped", bufs=4, align_bytes=64)
             h0, h1 = halves[0], halves[-1] + 1
-            nc.vector.tensor_copy(
-                out=grouped[key][:, 1024 * h0 : 1024 * h1].rearrange("p (tf m j) -> p m j tf", m=128, j=4),
-                in_=src.rearrange("p j (m tf) -> p m j tf", tf=4)[:, :, :, 2 * h0 : 2 * h1])
+            dst = grouped[key][:, 1024 * h0 : 1024 * h1].rearrange("p (tf m j) -> p m j tf", m=128, j=4)
+            src = src.rearrange("p j (m tf) -> p m j tf", tf=4)[:, :, :, 2 * h0 : 2 * h1]
+            if negate:
+                nc.vector.tensor_scalar(out=dst, in0=src, scalar1=-1.0, scalar2=None, op0=ALU.mult)
+            else:
+                nc.vector.tensor_copy(out=dst, in_=src)
 
         def ss_il(k, u, halves=(0, 1)):
             weave_in(("s", k, u), wide[k, u][:], halves)
@@ -149,20 +145,20 @@ def tile_learnedstencilwenostep_d1p_kernel(
             nc.vector.quantize_mx(out=ssq[:, k, u, 256 * h0 : 256 * h1].bitcast(FP8X4), scales=sss[:, k, u, 256 * h0 : 256 * h1], in_=grouped["s", k, u][:, 1024 * h0 : 1024 * h1])
 
         def cs_il(k, u):
-            weave_in(("c", k, u), cb[:, k, :, 512 * u : 512 * u + 512])
+            weave_in(("c", k, u), cb[:, k, :, 512 * u : 512 * u + 512], negate=(k == 0))
 
         def cs_q(k, u):
             nc.vector.quantize_mx(out=csq[:, k, u, :].bitcast(FP8X4), scales=css[:, k, u, :], in_=grouped["c", k, u][:])
 
-        def mm(dst, w, wsc, k, u, t, sign, c0, c1, start, stop):
+        def mm(dst, w, wsc, k, u, t, c0, c1, start, stop):
             nc.tensor.matmul_mx(
                 out=dst, lhsT=w[:, k, u, 128 * t : 128 * t + 128].bitcast(FP8X4), lhsT_scale=wsc[:, k, u, 128 * t : 128 * t + 128],
-                rhs=xq[:, sign, c0:c1].bitcast(FP8X4), rhs_scale=xs[:, sign, c0:c1], start=start, stop=stop)
+                rhs=xq[:, c0:c1].bitcast(FP8X4), rhs_scale=xs[:, c0:c1], start=start, stop=stop)
 
         def a_sq(u, t, k, h, eng="S"):
             c0, c1 = 512 * h, 512 * h + 512
             ps = psum.tile([P, 512], F32, name="sbank", tag="s", bufs=4)
-            mm(ps[:], ssq, sss, k, u, t, 0, c0, c1, True, True)
+            mm(ps[:], ssq, sss, k, u, t, c0, c1, True, True)
             dst = lg[:, k, u, t, c0:c1]
             if eng == "S":
                 nc.scalar.activation(out=dst, in_=ps[:], func=ACT.Square)
@@ -183,73 +179,64 @@ def tile_learnedstencilwenostep_d1p_kernel(
             e.tensor_tensor(out=lg[:, 0, u, t, :], in0=lg[:, 0, u, t, :], in1=lg[:, 1, u, t, :], op=ALU.subtract)
 
         def zone(unit):
-            if unit[0] == "t":
-                return lg[:, 0, unit[1], unit[2], 512 * unit[3] : 512 * unit[3] + 512]
-            return lg[:, 0, unit[1], :, 128 * unit[2] : 128 * unit[2] + 128]
+            u, t0, nt, c0, n = unit
+            return lg[:, 0, u, t0 : t0 + nt, c0 : c0 + n]
 
-        def like(unit, ap):
-            return ap if unit[0] == "t" else ap.rearrange("p (t b) -> p t b", t=4)
+        def like(unit, bank):
+            return bank[:].rearrange("p (t b) -> p t b", t=unit[2])
 
         def sig(unit):
             nc.scalar.activation(out=zone(unit), in_=zone(unit), func=ACT.Sigmoid, scale=2.0)
 
         def b_mm(unit):
-            u = unit[1]
+            u, t0, nt, c0, n = unit
             qb = psum.tile([P, 512], F32, name="qbank", tag="q", bufs=2)
             db = psum.tile([P, 512], F32, name="dbank", tag="d", bufs=2)
-            if unit[0] == "t":
-                jobs = [(unit[2], 0, 512, 512 * unit[3])]
-            else:
-                jobs = [(t, 128 * t, 128, 128 * unit[2]) for t in range(4)]
-            for t, o, n, c0 in jobs:
-                mm(db[:, o : o + n], csq, css, 1, u, t, 0, c0, c0 + n, True, False)
-                mm(db[:, o : o + n], csq, css, 0, u, t, 1, c0, c0 + n, False, True)
-            for t, o, n, c0 in jobs:
-                mm(qb[:, o : o + n], csq, css, 0, u, t, 0, c0, c0 + n, True, True)
+            for t in range(nt):
+                mm(db[:, t * n : t * n + n], csq, css, 1, u, t0 + t, c0, c0 + n, True, False)
+                mm(db[:, t * n : t * n + n], csq, css, 0, u, t0 + t, c0, c0 + n, False, True)
+            for t in range(nt):
+                mm(qb[:, t * n : t * n + n], csq, css, 0, u, t0 + t, c0, c0 + n, True, True)
             st["q", unit], st["d", unit] = qb, db
 
         def b_td(unit):
-            nc.vector.tensor_tensor(out=zone(unit), in0=like(unit, st["d", unit][:]), in1=zone(unit), op=ALU.mult)
+            nc.vector.tensor_tensor(out=zone(unit), in0=like(unit, st["d", unit]), in1=zone(unit), op=ALU.mult)
 
-        def b_qh(unit):
-            nc.vector.tensor_tensor(out=zone(unit), in0=like(unit, st["q", unit][:]), in1=zone(unit), op=ALU.add)
+        def b_qh(unit, flux="S"):
+            if flux == "G":
+                nc.vector.scalar_tensor_tensor(out=zone(unit), in0=zone(unit), scalar=1.0, in1=like(unit, st["q", unit]), op0=ALU.add, op1=ALU.subtract)
+                return
+            nc.vector.tensor_tensor(out=zone(unit), in0=zone(unit), in1=like(unit, st["q", unit]), op=ALU.subtract)
 
         def b_flux(unit, eng):
             v = zone(unit)
-            if eng == "S":
-                nc.scalar.activation(out=v, in_=v, func=ACT.Square, bias=1.0)
-            else:
+            if eng == "V":
                 nc.vector.scalar_tensor_tensor(out=v, in0=v, scalar=2.0, in1=v, op0=ALU.add, op1=ALU.mult)
+            elif eng == "G":
+                nc.gpsimd.tensor_tensor(out=v, in0=v, in1=v, op=ALU.mult)
+            else:
+                nc.scalar.activation(out=v, in_=v, func=ACT.Square, bias=1.0)
 
         def b_fin(unit, eng):
-            u = unit[1]
-            if unit[0] == "t":
-                if unit[2] == 0:
-                    st["pt", u, unit[3]] = work.tile([P, 4, 512], BF16, name="pgt", tag="pgt", bufs=2)
-                jobs = [(unit[2], st["pt", u, unit[3]][:, unit[2], :], zone(unit))]
-            else:
-                st["pi", unit[2]] = work.tile([P, 4, 128], BF16, name="pgi", tag="pgi", bufs=2)
-                jobs = [(t, st["pi", unit[2]][:, t, :], zone(unit)[:, t, :]) for t in range(4)]
-            for t, dst, src in jobs:
-                if eng == "S":
-                    nc.vector.tensor_scalar(out=dst, in0=src, scalar1=gh[:, u, t : t + 1], scalar2=ghn[:, u, t : t + 1], op0=ALU.mult, op1=ALU.add)
+            u, t0, nt, c0, n = unit
+            if t0 == 0:
+                st["pt", u, c0] = work.tile([P, 4, n], BF16, name="pgt", tag="pgt" + str(n), bufs=2)
+            dst = st["pt", u, c0]
+            for t in range(t0, t0 + nt):
+                src = lg[:, 0, u, t, c0 : c0 + n]
+                if eng == "V":
+                    nc.vector.tensor_scalar(out=dst[:, t, :], in0=src, scalar1=gh[:, u, t : t + 1], scalar2=None, op0=ALU.mult)
+                elif eng in "SG":
+                    nc.vector.tensor_scalar(out=dst[:, t, :], in0=src, scalar1=gh[:, u, t : t + 1], scalar2=ghn[:, u, t : t + 1], op0=ALU.mult, op1=ALU.add)
                 else:
-                    nc.vector.tensor_scalar(out=dst, in0=src, scalar1=gh[:, u, t : t + 1], scalar2=None, op0=ALU.mult)
+                    nc.scalar.activation(out=dst[:, t, :], in_=src, func=ACT.Identity, scale=gh[:, u, t : t + 1], bias=ghn[:, u, t : t + 1])
 
-        def span(unit):
-            return (512 * unit[3], 512) if unit[0] == "t" else (128 * unit[2], 128)
-
-        def b_il(unit):
-            u = unit[1]
-            c0, n = span(unit)
-            src = st["pt", u, unit[3]] if unit[0] == "t" else st["pi", unit[2]]
+        def b_il(u, c0, n):
             nc.vector.tensor_copy(
                 out=pg[:, u, 4 * c0 : 4 * (c0 + n)].rearrange("p (c i t) -> p c t i", i=4, t=4),
-                in_=src[:].rearrange("p t (c i) -> p c t i", i=4))
+                in_=st["pt", u, c0][:].rearrange("p t (c i) -> p c t i", i=4))
 
-        def b_quant(unit):
-            u = unit[1]
-            c0, n = span(unit)
+        def b_quant(u, c0, n):
             nc.vector.quantize_mx(out=pq[:, u, c0 : c0 + n].bitcast(FP8X4), scales=ps8[:, u, c0 : c0 + n], in_=pg[:, u, 4 * c0 : 4 * (c0 + n)])
 
         def b_out(i):
@@ -270,40 +257,37 @@ def tile_learnedstencilwenostep_d1p_kernel(
 
 
         FLUX0 = "VVVVVVVV"
-        FLUX1 = "SSSSSSSS"
+        FLUX1 = "IIIISSSS"
         SUB1 = "VVVV"
-        EVAC = "SSSSSSSS"
-        widen(0, 0, "S", (0, 1))
-        widen(0, 0, "V", (2, 3))
+        for t in range(4):
+            widen(0, 0, "SSVV"[t], (t,))
         turn_x(0, "S")
         ss_il(0, 0, (0,))
         turn_x(1, "S")
         ss_q(0, 0, (0,))
         ss_il(0, 0, (1,))
-        quant_x(0, 0, 4)
+        quant_x(0, 4)
         ss_q(0, 0, (1,))
         for t in range(4):
-            widen(1, 0, "SSSS"[t], (t,))
+            widen(1, 0, "SVVV"[t], (t,))
         for t in range(2):
             a_sq(0, t, 0, 0)
-        ss_il(1, 0)
         turn_x(2, "S")
         turn_x(3, "S")
         for t in range(2, 4):
             a_sq(0, t, 0, 0)
+        ss_il(1, 0)
+        quant_x(4, 8)
         ss_q(1, 0)
-        quant_x(0, 4, 8)
-        for t in range(4):
-            a_sq(0, t, 1, 0)
         for t in range(4):
             a_sq(0, t, 0, 1)
+        for t in range(4):
+            a_sq(0, t, 1, 0)
             a_sq(0, t, 1, 1)
         for t in range(4):
             for k in range(2):
                 a_ln(0, t, k)
-        negate_x(0, 4)
         cs_il(0, 0)
-        quant_x(1, 0, 4)
         cs_il(1, 0)
         cs_q(0, 0)
         widen(0, 1, "V")
@@ -312,21 +296,29 @@ def tile_learnedstencilwenostep_d1p_kernel(
         widen(1, 1, "V")
         ss_q(0, 1)
         ss_il(1, 1)
-        negate_x(4, 8)
+        cs_il(0, 1)
         ss_q(1, 1)
-        quant_x(1, 4, 8)
+        cs_q(0, 1)
         for t in range(4):
-            a_sub(0, t, "V")
+            a_sub(0, t, "VVVV"[t])
+        def make_units(u, groups):
+            res, c0 = [], 0
+            for n in groups:
+                nt = 512 // n
+                res += [(u, t0, nt, c0, n) for t0 in range(0, 4, nt)]
+                c0 += n
+            return res
 
-        units0 = [("t", 0, t, h) for h in range(2) for t in range(4)]
-        units1 = [("t", 1, t, 0) for t in range(4)] + [("i", 1, i) for i in range(4, 8)]
+        def last_of(unit):
+            return unit[1] + unit[2] == 4
+
+        units0 = make_units(0, (512, 512))
+        units1 = make_units(1, (256, 256, 256, 256))
         for unit in units0:
             sig(unit)
         b_mm(units0[0])
         extra = [
-            lambda: cs_il(0, 1),
             lambda: cs_il(1, 1),
-            lambda: cs_q(0, 1),
             lambda: cs_q(1, 1),
         ]
         for m in range(TILES + 4):
@@ -339,57 +331,55 @@ def tile_learnedstencilwenostep_d1p_kernel(
             if m < TILES:
                 b_td(units0[m])
             if 0 <= m - 1 < TILES:
-                b_qh(units0[m - 1])
+                b_qh(units0[m - 1], FLUX0[m - 1])
             if m + 1 < TILES:
                 b_mm(units0[m + 1])
             if 0 <= m - 2 < TILES:
                 b_flux(units0[m - 2], FLUX0[m - 2])
             if 0 <= m - 3 < TILES:
                 b_fin(units0[m - 3], FLUX0[m - 3])
-            if 3 <= m < 3 + 4:
+            if 3 <= m < 3 + 2:
                 extra[m - 3]()
             if m in (7, 11):
-                b_il(units0[m - 4])
+                b_il(0, 512 * (m // 11), 512)
             if m == 8:
-                b_quant(units0[3])
+                b_quant(0, 0, 512)
             if m >= 6 and m % 2 == 6 % 2 and (m - 6) // 2 < 3:
                 a_sub(1, (m - 6) // 2, SUB1[(m - 6) // 2])
         for t in range(4):
             if 2 * t + 6 >= TILES + 4 or t == 3:
                 a_sub(1, t, SUB1[t])
-        sig(units1[0])
-        sig(units1[1])
+        for unit in units1[:2]:
+            sig(unit)
         b_mm(units1[0])
-        b_quant(units0[7])
+        b_quant(0, 512, 512)
         EVACS = "SSSSSSSS"
         outs = []
-        for m in range(TILES + 5):
-            if m < TILES:
+        total = len(units1)
+        for m in range(total + 5):
+            if m < total:
                 b_td(units1[m])
-            if 0 <= m - 1 < TILES:
-                b_qh(units1[m - 1])
-            if m + 1 < TILES:
+            if 0 <= m - 1 < total:
+                b_qh(units1[m - 1], FLUX1[m - 1])
+            if m + 1 < total:
                 b_mm(units1[m + 1])
-            if 0 <= m - 2 < TILES:
+            if 0 <= m - 2 < total:
                 b_flux(units1[m - 2], FLUX1[m - 2])
-            if m + 2 < TILES:
+            if m + 2 < total:
                 sig(units1[m + 2])
             for _ in range(2):
                 if outs and outs[0][0] < m:
                     i = outs.pop(0)[1]
                     b_evac(i, EVACS[i])
-            if m >= 7 and m - 4 < TILES:
-                b_il(units1[m - 4])
-            if 0 <= m - 3 < TILES:
+            done = units1[m - 4] if 0 <= m - 4 < total and last_of(units1[m - 4]) else None
+            if done:
+                b_il(1, done[3], done[4])
+            if 0 <= m - 3 < total:
                 b_fin(units1[m - 3], FLUX1[m - 3])
-            if m == 7:
-                b_quant(units1[3])
-                outs += [(m, i) for i in range(4)]
-                for i in range(4):
+            if done:
+                b_quant(1, done[3], done[4])
+                for i in range(done[3] // 128, (done[3] + done[4]) // 128):
                     b_out(i)
-            if 8 <= m and m - 4 < TILES:
-                b_quant(units1[m - 4])
-                b_out(m - 4)
-                outs.append((m, m - 4))
+                    outs.append((m, i))
         for m, i in outs:
             b_evac(i, EVACS[i])

@@ -49,33 +49,28 @@ def tile_learnedstencilwenostep_d1p_kernel(
         dvs = keep.tile([P, 2, 512], U8, name="dvs", align_bytes=64)
         gmb = keep.tile([P, 2, 2, 4], BF16, name="gmb")
         gb = keep.tile([P, 2, 4], BF16, name="gb")
-        gmf = keep.tile([P, 16], F32, name="gmf")
-        half = keep.tile([P, 16], F32, name="half")
-        rt = keep.tile([P, 16], F32, name="rt")
-        rth = keep.tile([P, 16], F32, name="rth")
+        lng = keep.tile([P, 2, 8], F32, name="lng")
+        bl = keep.tile([P, 8], F32, name="bl")
         gh = keep.tile([P, 2, 4], F32, name="gh")
         ident = keep.tile([P, P], F32, name="ident")
-        warm = keep.tile([P, 1], F32, name="warm")
 
         xv = x.rearrange("(p i) d -> p i d", i=TILES)
         ov = out.rearrange("(p i) d -> p i d", i=TILES)
 
         sv = [ss_bytes[k].rearrange("(p t) n -> p t n", t=4) for k in range(2)]
+        nc.scalar.dma_start(out=gmb[:].rearrange("p k u t -> p (k u) t"), in_=gamma.rearrange("k (u p t) -> p (k u) t", p=P, t=4))
         nc.scalar.dma_start(out=scl[:], in_=ss_scale.rearrange("k (p t) j -> p k (t j)", t=4))
         nc.sync.dma_start(out=sb[:, 0, :, 0:512], in_=sv[0][:, :, 0:512])
         nc.sync.dma_start(out=xr[:, 0:4, :], in_=xv[:, 0:4, :])
-        nc.sync.dma_start(out=sb[:, 1, :, 0:512], in_=sv[1][:, :, 0:512])
+        nc.sync.dma_start(out=sb[:, 1, :, :], in_=sv[1])
         nc.sync.dma_start(out=xr[:, 4:8, :], in_=xv[:, 4:8, :])
-        nc.scalar.dma_start(out=gmb[:].rearrange("p k u t -> p (k u) t"), in_=gamma.rearrange("k (u p t) -> p (k u) t", p=P, t=4))
-        nc.scalar.dma_start(out=gb[:], in_=g.rearrange("(u p t) -> p u t", p=P, t=4))
-        for k in range(2):
-            nc.sync.dma_start(out=sb[:, k, :, 512:1024], in_=sv[k][:, :, 512:1024])
+        nc.sync.dma_start(out=sb[:, 0, :, 512:1024], in_=sv[0][:, :, 512:1024])
+        nc.sync.dma_start(out=gb[:], in_=g.rearrange("(u p t) -> p u t", p=P, t=4))
         for k in range(2):
             nc.sync.dma_start(out=cb[:, k, :, :], in_=cs[k].rearrange("(p t) n -> p t n", t=4))
         nc.sync.dma_start(out=dvw[:].bitcast(I32), in_=dv_words.rearrange("g p n -> p g n").bitcast(I32))
 
-        nc.vector.memset(warm[:], 1.0)
-        nc.scalar.activation(out=warm[:], in_=warm[:], func=ACT.Ln)
+        nc.scalar.activation(out=lng[:].rearrange("p k v -> p (k v)"), in_=gmb[:].rearrange("p k u t -> p (k u t)"), func=ACT.Ln, bias=1e-18)
         make_identity(nc, ident[:])
         nc.vector.memset(dvs[:].rearrange("p g n -> p (g n)").bitcast(I32), 0)
         for q in range(4):
@@ -83,17 +78,10 @@ def tile_learnedstencilwenostep_d1p_kernel(
                 out=dvs[32 * q : 32 * q + 4, :, :].bitcast(I32),
                 in_=dv_scales[:, 4 * q : 4 * q + 4, :].rearrange("g r n -> r g n").bitcast(I32),
             )
-        nc.gpsimd.memset(half[:], 0.5)
-        nc.gpsimd.tensor_scalar(out=gmf[:], in0=gmb[:].rearrange("p k u t -> p (k u t)"), scalar1=1e-30, scalar2=None, op0=ALU.max)
-        nc.gpsimd.tensor_tensor(out=rt[:], in0=gmf[:], in1=half[:], op=ALU.pow)
-        nc.gpsimd.tensor_scalar(out=rth[:], in0=rt[:], scalar1=0.5, scalar2=None, op0=ALU.mult)
-        nc.gpsimd.tensor_scalar(out=gh[:].rearrange("p u t -> p (u t)"), in0=gb[:].rearrange("p u t -> p (u t)"), scalar1=0.5, scalar2=None, op0=ALU.mult)
-        nc.gpsimd.tensor_scalar(out=ghn[:].rearrange("p u t -> p (u t)"), in0=gb[:].rearrange("p u t -> p (u t)"), scalar1=-0.5, scalar2=None, op0=ALU.mult)
-
         words = xr[:].rearrange("p i d -> p (i d)").bitcast(F32)
 
         def turn_x(pair, eng):
-            bank = psum.tile([P, 2, 2, 128], F32, tag="dq"[pair % 2], name="xbank", bufs=2)
+            bank = psum.tile([P, 2, 2, 128], F32, tag="dq"[pair % 2], name="xbank", bufs=3 - pair % 2)
             for ii in range(2):
                 i = 2 * pair + ii
                 for u in range(2):
@@ -157,7 +145,7 @@ def tile_learnedstencilwenostep_d1p_kernel(
 
         def a_sq(u, t, k, h, eng="S"):
             c0, c1 = 512 * h, 512 * h + 512
-            ps = psum.tile([P, 512], F32, name="sbank", tag="s", bufs=4)
+            ps = psum.tile([P, 512], F32, name="sbank", tag="s", bufs=3)
             mm(ps[:], ssq, sss, k, u, t, c0, c1, True, True)
             dst = lg[:, k, u, t, c0:c1]
             if eng == "S":
@@ -170,9 +158,14 @@ def tile_learnedstencilwenostep_d1p_kernel(
             nc.vector.tensor_tensor(out=dst, in0=dst, in1=dst, op=ALU.mult)
 
         def a_ln(u, t, k):
-            j = 8 * (1 - k) + 4 * u + t
             v = lg[:, k, u, t, :]
-            nc.scalar.activation(out=v, in_=v, func=ACT.Ln, bias=rth[:, j : j + 1], scale=rt[:, j : j + 1])
+            nc.scalar.activation(out=v, in_=v, func=ACT.Ln, bias=0.5)
+
+        def consts():
+            nc.vector.tensor_tensor(out=bl[:], in0=lng[:, 1, :], in1=lng[:, 0, :], op=ALU.subtract)
+            gflat = gb[:].rearrange("p u t -> p (u t)")
+            nc.vector.tensor_scalar(out=gh[:].rearrange("p u t -> p (u t)"), in0=gflat, scalar1=0.5, scalar2=None, op0=ALU.mult)
+            nc.vector.tensor_scalar(out=ghn[:].rearrange("p u t -> p (u t)"), in0=gflat, scalar1=-0.5, scalar2=None, op0=ALU.mult)
 
         def a_sub(u, t, eng):
             e = nc.vector if eng == "V" else nc.gpsimd
@@ -185,19 +178,25 @@ def tile_learnedstencilwenostep_d1p_kernel(
         def like(unit, bank):
             return bank[:].rearrange("p (t b) -> p t b", t=unit[2])
 
-        def sig(unit):
-            nc.scalar.activation(out=zone(unit), in_=zone(unit), func=ACT.Sigmoid, scale=2.0)
+        def sig(u, j):
+            h, t = divmod(j, 4)
+            v = lg[:, 0, u, t, 512 * h : 512 * h + 512]
+            nc.scalar.activation(out=v, in_=v, func=ACT.Sigmoid, scale=2.0, bias=bl[:, 4 * u + t : 4 * u + t + 1])
 
-        def b_mm(unit):
+        def b_mm_d(unit):
             u, t0, nt, c0, n = unit
-            qb = psum.tile([P, 512], F32, name="qbank", tag="q", bufs=2)
-            db = psum.tile([P, 512], F32, name="dbank", tag="d", bufs=2)
+            db = psum.tile([P, 512], F32, name="dbank", tag="d", bufs=3)
             for t in range(nt):
                 mm(db[:, t * n : t * n + n], csq, css, 1, u, t0 + t, c0, c0 + n, True, False)
                 mm(db[:, t * n : t * n + n], csq, css, 0, u, t0 + t, c0, c0 + n, False, True)
+            st["d", unit] = db
+
+        def b_mm_q(unit):
+            u, t0, nt, c0, n = unit
+            qb = psum.tile([P, 512], F32, name="qbank", tag="q", bufs=2)
             for t in range(nt):
                 mm(qb[:, t * n : t * n + n], csq, css, 0, u, t0 + t, c0, c0 + n, True, True)
-            st["q", unit], st["d", unit] = qb, db
+            st["q", unit] = qb
 
         def b_td(unit):
             nc.vector.tensor_tensor(out=zone(unit), in0=like(unit, st["d", unit]), in1=zone(unit), op=ALU.mult)
@@ -240,7 +239,7 @@ def tile_learnedstencilwenostep_d1p_kernel(
             nc.vector.quantize_mx(out=pq[:, u, c0 : c0 + n].bitcast(FP8X4), scales=ps8[:, u, c0 : c0 + n], in_=pg[:, u, 4 * c0 : 4 * (c0 + n)])
 
         def b_out(i):
-            ob = psum.tile([P, 512], F32, name="obank", tag="s", bufs=4)
+            ob = psum.tile([P, 512], F32, name="obank", tag="s", bufs=3)
             for u in range(2):
                 nc.tensor.matmul_mx(
                     out=ob[:], lhsT=pq[:, u, 128 * i : 128 * i + 128].bitcast(FP8X4), lhsT_scale=ps8[:, u, 128 * i : 128 * i + 128],
@@ -248,7 +247,7 @@ def tile_learnedstencilwenostep_d1p_kernel(
             st["o", i] = ob
 
         def b_evac(i, eng):
-            ot = work.tile([P, 512], F32, name="ot", tag="ot", bufs=4)
+            ot = work.tile([P, 512], F32, name="ot", tag="ot", bufs=8)
             if eng == "S":
                 nc.scalar.copy(out=ot[:], in_=st["o", i][:])
             else:
@@ -257,10 +256,20 @@ def tile_learnedstencilwenostep_d1p_kernel(
 
 
         FLUX0 = "VVVVVVVV"
-        FLUX1 = "IIIISSSS"
+        FLUX1 = "IIIIISSSS"
+        SUB0 = "VVVV"
         SUB1 = "VVVV"
+        EVACS = "SSSSSSSS"
+        VSQ = ()
+
+        def square(u, t, k, h):
+            onv = (u, t, k, h) in VSQ
+            a_sq(u, t, k, h, "V" if onv else "S")
+            if onv:
+                a_mul(u, t, k, h)
+
         for t in range(4):
-            widen(0, 0, "SSVV"[t], (t,))
+            widen(0, 0, "SVVV"[t], (t,))
         turn_x(0, "S")
         ss_il(0, 0, (0,))
         turn_x(1, "S")
@@ -271,36 +280,38 @@ def tile_learnedstencilwenostep_d1p_kernel(
         for t in range(4):
             widen(1, 0, "SVVV"[t], (t,))
         for t in range(2):
-            a_sq(0, t, 0, 0)
+            square(0, t, 0, 0)
         turn_x(2, "S")
         turn_x(3, "S")
         for t in range(2, 4):
-            a_sq(0, t, 0, 0)
+            square(0, t, 0, 0)
         ss_il(1, 0)
         quant_x(4, 8)
         ss_q(1, 0)
         for t in range(4):
-            a_sq(0, t, 0, 1)
+            square(0, t, 0, 1)
         for t in range(4):
-            a_sq(0, t, 1, 0)
-            a_sq(0, t, 1, 1)
+            square(0, t, 1, 0)
+            square(0, t, 1, 1)
         for t in range(4):
             for k in range(2):
                 a_ln(0, t, k)
-        cs_il(0, 0)
-        cs_il(1, 0)
-        cs_q(0, 0)
         widen(0, 1, "V")
-        cs_q(1, 0)
         ss_il(0, 1)
         widen(1, 1, "V")
         ss_q(0, 1)
         ss_il(1, 1)
-        cs_il(0, 1)
+        cs_il(0, 0)
         ss_q(1, 1)
+        cs_il(1, 0)
+        cs_q(0, 0)
+        cs_il(0, 1)
+        cs_q(1, 0)
         cs_q(0, 1)
+        consts()
         for t in range(4):
-            a_sub(0, t, "VVVV"[t])
+            a_sub(0, t, SUB0[t])
+
         def make_units(u, groups):
             res, c0 = [], 0
             for n in groups:
@@ -313,10 +324,12 @@ def tile_learnedstencilwenostep_d1p_kernel(
             return unit[1] + unit[2] == 4
 
         units0 = make_units(0, (512, 512))
-        units1 = make_units(1, (256, 256, 256, 256))
-        for unit in units0:
-            sig(unit)
-        b_mm(units0[0])
+        units1 = make_units(1, (256, 256, 256, 128, 128))
+        for j in range(8):
+            sig(0, j)
+        b_mm_d(units0[0])
+        b_mm_q(units0[0])
+        b_mm_d(units0[1])
         extra = [
             lambda: cs_il(1, 1),
             lambda: cs_q(1, 1),
@@ -325,15 +338,17 @@ def tile_learnedstencilwenostep_d1p_kernel(
             n = m - 2
             if 0 <= n < TILES:
                 for h in range(2):
-                    a_sq(1, n // 2, n % 2, h)
+                    square(1, n // 2, n % 2, h)
             if 1 <= n < TILES + 1:
                 a_ln(1, (n - 1) // 2, (n - 1) % 2)
             if m < TILES:
                 b_td(units0[m])
+            if m + 2 < TILES:
+                b_mm_d(units0[m + 2])
             if 0 <= m - 1 < TILES:
                 b_qh(units0[m - 1], FLUX0[m - 1])
             if m + 1 < TILES:
-                b_mm(units0[m + 1])
+                b_mm_q(units0[m + 1])
             if 0 <= m - 2 < TILES:
                 b_flux(units0[m - 2], FLUX0[m - 2])
             if 0 <= m - 3 < TILES:
@@ -349,26 +364,29 @@ def tile_learnedstencilwenostep_d1p_kernel(
         for t in range(4):
             if 2 * t + 6 >= TILES + 4 or t == 3:
                 a_sub(1, t, SUB1[t])
-        for unit in units1[:2]:
-            sig(unit)
-        b_mm(units1[0])
+        for j in range(5):
+            sig(1, j)
+        b_mm_d(units1[0])
+        b_mm_q(units1[0])
+        b_mm_d(units1[1])
         b_quant(0, 512, 512)
-        EVACS = "SSSSSSSS"
         outs = []
         total = len(units1)
         for m in range(total + 5):
             if m < total:
                 b_td(units1[m])
+            if m + 2 < total:
+                b_mm_d(units1[m + 2])
             if 0 <= m - 1 < total:
                 b_qh(units1[m - 1], FLUX1[m - 1])
             if m + 1 < total:
-                b_mm(units1[m + 1])
+                b_mm_q(units1[m + 1])
             if 0 <= m - 2 < total:
                 b_flux(units1[m - 2], FLUX1[m - 2])
-            if m + 2 < total:
-                sig(units1[m + 2])
-            for _ in range(2):
-                if outs and outs[0][0] < m:
+            if m + 5 < 8:
+                sig(1, m + 5)
+            for _ in range(1):
+                if outs and outs[0][0] <= m - 2:
                     i = outs.pop(0)[1]
                     b_evac(i, EVACS[i])
             done = units1[m - 4] if 0 <= m - 4 < total and last_of(units1[m - 4]) else None

from contextlib import ExitStack

import concourse.mybir as mybir
from concourse.masks import make_identity

F32 = mybir.dt.float32
BF16 = mybir.dt.bfloat16
I32 = mybir.dt.int32
U32 = mybir.dt.uint32
U8 = mybir.dt.uint8
FP8 = mybir.dt.float8_e4m3fn
FP8X4 = mybir.dt.float8_e4m3fn_x4
FP4X4 = mybir.dt.float4_e2m1fn_x4
ALU = mybir.AluOpType
ACT = mybir.ActivationFunctionType

FLOPS = 2 * 5 * 1024 * 512 * 1024
P = 128
TILES = 8


def tile_learnedstencilwenostep_d1p_kernel(
    tc, x, cs, ss_bytes, ss_scale, gamma, g, dv_words, dv_scales, out
):
    nc = tc.nc
    with ExitStack() as ctx:
        ctx.enter_context(tc.manual_schedule())
        keep = ctx.enter_context(tc.tile_pool(name="keep", bufs=1))
        work = ctx.enter_context(tc.tile_pool(name="work", bufs=2))
        psum = ctx.enter_context(tc.psum_pool(name="psum", bufs=1))

        xr = keep.tile([P, TILES, 512], BF16, name="xr")
        xt = keep.tile([P, TILES, 128, 4], BF16, name="xt", align_bytes=64)
        xq = keep.tile([P, 1024], U32, name="xq", align_bytes=64)
        xs = keep.tile([P, 1024], U8, name="xs", align_bytes=64)
        sb = keep.tile([P, 2, 4, 1024], U8, name="sb", align_bytes=64)
        scl = keep.tile([P, 2, 32], F32, name="scl")
        ssq = keep.tile([P, 2, 2, 512], U32, name="ssq", align_bytes=64)
        sss = keep.tile([P, 2, 2, 512], U8, name="sss", align_bytes=64)
        cb = keep.tile([P, 2, 4, 1024], BF16, name="cb", align_bytes=64)
        csq = keep.tile([P, 2, 2, 512], U32, name="csq", align_bytes=64)
        css = keep.tile([P, 2, 2, 512], U8, name="css", align_bytes=64)
        lg = keep.tile([P, 2, 2, 4, 1024], F32, name="lg")
        pg = keep.tile([P, 2, 4096], BF16, name="pg", align_bytes=64)
        pq = keep.tile([P, 2, 1024], U32, name="pq", align_bytes=64)
        ps8 = keep.tile([P, 2, 1024], U8, name="ps8", align_bytes=64)
        ghn = keep.tile([P, 2, 4], F32, name="ghn")
        dvw = keep.tile([P, 2, 1024], U8, name="dvw", align_bytes=64)
        dvs = keep.tile([P, 2, 512], U8, name="dvs", align_bytes=64)
        gmb = keep.tile([P, 2, 2, 4], BF16, name="gmb")
        gb = keep.tile([P, 2, 4], BF16, name="gb")
        lng = keep.tile([P, 2, 8], F32, name="lng")
        bl = keep.tile([P, 8], F32, name="bl")
        gh = keep.tile([P, 2, 4], F32, name="gh")
        ident = keep.tile([P, P], F32, name="ident")

        xv = x.rearrange("(p i) d -> p i d", i=TILES)
        ov = out.rearrange("(p i) d -> p i d", i=TILES)

        sv = [ss_bytes[k].rearrange("(p t) n -> p t n", t=4) for k in range(2)]
        nc.scalar.dma_start(out=gmb[:].rearrange("p k u t -> p (k u) t"), in_=gamma.rearrange("k (u p t) -> p (k u) t", p=P, t=4))
        nc.scalar.dma_start(out=scl[:], in_=ss_scale.rearrange("k (p t) j -> p k (t j)", t=4))
        nc.sync.dma_start(out=sb[:, 0, :, 0:512], in_=sv[0][:, :, 0:512])
        nc.sync.dma_start(out=xr[:, 0:4, :], in_=xv[:, 0:4, :])
        nc.sync.dma_start(out=sb[:, 1, :, :], in_=sv[1])
        nc.sync.dma_start(out=xr[:, 4:8, :], in_=xv[:, 4:8, :])
        nc.sync.dma_start(out=sb[:, 0, :, 512:1024], in_=sv[0][:, :, 512:1024])
        nc.sync.dma_start(out=gb[:], in_=g.rearrange("(u p t) -> p u t", p=P, t=4))
        for k in range(2):
            nc.sync.dma_start(out=cb[:, k, :, :], in_=cs[k].rearrange("(p t) n -> p t n", t=4))
        nc.sync.dma_start(out=dvw[:].bitcast(I32), in_=dv_words.rearrange("g p n -> p g n").bitcast(I32))

        nc.scalar.activation(out=lng[:].rearrange("p k v -> p (k v)"), in_=gmb[:].rearrange("p k u t -> p (k u t)"), func=ACT.Ln, bias=1e-18)
        make_identity(nc, ident[:])
        nc.vector.memset(dvs[:].rearrange("p g n -> p (g n)").bitcast(I32), 0)
        for q in range(4):
            nc.sync.dma_start(
                out=dvs[32 * q : 32 * q + 4, :, :].bitcast(I32),
                in_=dv_scales[:, 4 * q : 4 * q + 4, :].rearrange("g r n -> r g n").bitcast(I32),
            )
        words = xr[:].rearrange("p i d -> p (i d)").bitcast(F32)

        def turn_x(pair, eng):
            bank = psum.tile([P, 2, 2, 128], F32, tag="dq"[pair % 2], name="xbank", bufs=3 - pair % 2)
            for ii in range(2):
                i = 2 * pair + ii
                for u in range(2):
                    nc.tensor.transpose(bank[:, ii, u, :], words[:, 256 * i + u : 256 * (i + 1) : 2], ident[:])
            dst = xt[:, 2 * pair : 2 * pair + 2, :, :].rearrange("p i r t -> p (i r t)").bitcast(F32).rearrange("p (i r u) -> p i r u", i=2, u=2)
            src = bank[:].rearrange("p i u r -> p i r u")
            if eng == "S":
                nc.scalar.copy(out=dst, in_=src)
            else:
                nc.vector.tensor_copy(out=dst, in_=src)

        def quant_x(t0, t1):
            src = xt[:, t0:t1, :, :].rearrange("p i r t -> p (i r t)")
            nc.vector.quantize_mx(out=xq[:, 128 * t0 : 128 * t1].bitcast(FP8X4), scales=xs[:, 128 * t0 : 128 * t1], in_=src)

        st = {}
        wide = {}
        grouped = {}

        def widen(k, u, eng, ts=range(4)):
            if (k, u) not in wide:
                wide[k, u] = work.tile([P, 4, 512], BF16, name="wide", tag="wide", bufs=3)
            for t in ts:
                for j in range(4):
                    dst = wide[k, u][:, t, 128 * j : 128 * j + 128]
                    src = sb[:, k, t, 512 * u + 128 * j : 512 * u + 128 * j + 128].bitcast(FP8)
                    col = 8 * t + 4 * u + j
                    if eng == "S":
                        nc.scalar.activation(out=dst, in_=src, func=ACT.Copy, scale=scl[:, k, col : col + 1])
                    else:
                        nc.vector.tensor_scalar(out=dst, in0=src, scalar1=scl[:, k, col : col + 1], scalar2=None, op0=ALU.mult)

        def weave_in(key, src, halves=(0, 1), negate=False):
            if key not in grouped:
                grouped[key] = work.tile([P, 2048], BF16, name="grouped", tag="grouped", bufs=4, align_bytes=64)
            h0, h1 = halves[0], halves[-1] + 1
            dst = grouped[key][:, 1024 * h0 : 1024 * h1].rearrange("p (tf m j) -> p m j tf", m=128, j=4)
            src = src.rearrange("p j (m tf) -> p m j tf", tf=4)[:, :, :, 2 * h0 : 2 * h1]
            if negate:
                nc.vector.tensor_scalar(out=dst, in0=src, scalar1=-1.0, scalar2=None, op0=ALU.mult)
            else:
                nc.vector.tensor_copy(out=dst, in_=src)

        def ss_il(k, u, halves=(0, 1)):
            weave_in(("s", k, u), wide[k, u][:], halves)

        def ss_q(k, u, halves=(0, 1)):
            h0, h1 = halves[0], halves[-1] + 1
            nc.vector.quantize_mx(out=ssq[:, k, u, 256 * h0 : 256 * h1].bitcast(FP8X4), scales=sss[:, k, u, 256 * h0 : 256 * h1], in_=grouped["s", k, u][:, 1024 * h0 : 1024 * h1])

        def cs_il(k, u):
            weave_in(("c", k, u), cb[:, k, :, 512 * u : 512 * u + 512], negate=(k == 0))

        def cs_q(k, u):
            nc.vector.quantize_mx(out=csq[:, k, u, :].bitcast(FP8X4), scales=css[:, k, u, :], in_=grouped["c", k, u][:])

        def mm(dst, w, wsc, k, u, t, c0, c1, start, stop):
            nc.tensor.matmul_mx(
                out=dst, lhsT=w[:, k, u, 128 * t : 128 * t + 128].bitcast(FP8X4), lhsT_scale=wsc[:, k, u, 128 * t : 128 * t + 128],
                rhs=xq[:, c0:c1].bitcast(FP8X4), rhs_scale=xs[:, c0:c1], start=start, stop=stop)

        def a_sq(u, t, k, h, eng="S"):
            c0, c1 = 512 * h, 512 * h + 512
            ps = psum.tile([P, 512], F32, name="sbank", tag="s", bufs=3)
            mm(ps[:], ssq, sss, k, u, t, c0, c1, True, True)
            dst = lg[:, k, u, t, c0:c1]
            if eng == "S":
                nc.scalar.activation(out=dst, in_=ps[:], func=ACT.Square)
            else:
                nc.vector.tensor_copy(out=dst, in_=ps[:])

        def a_mul(u, t, k, h):
            dst = lg[:, k, u, t, 512 * h : 512 * h + 512]
            nc.vector.tensor_tensor(out=dst, in0=dst, in1=dst, op=ALU.mult)

        def a_ln(u, t, k):
            v = lg[:, k, u, t, :]
            nc.scalar.activation(out=v, in_=v, func=ACT.Ln, bias=0.5)

        def consts():
            nc.vector.tensor_tensor(out=bl[:], in0=lng[:, 1, :], in1=lng[:, 0, :], op=ALU.subtract)
            gflat = gb[:].rearrange("p u t -> p (u t)")
            nc.vector.tensor_scalar(out=gh[:].rearrange("p u t -> p (u t)"), in0=gflat, scalar1=0.5, scalar2=None, op0=ALU.mult)
            nc.vector.tensor_scalar(out=ghn[:].rearrange("p u t -> p (u t)"), in0=gflat, scalar1=-0.5, scalar2=None, op0=ALU.mult)

        def a_sub(u, t, eng):
            e = nc.vector if eng == "V" else nc.gpsimd
            e.tensor_tensor(out=lg[:, 0, u, t, :], in0=lg[:, 0, u, t, :], in1=lg[:, 1, u, t, :], op=ALU.subtract)

        def zone(unit):
            u, t0, nt, c0, n = unit
            return lg[:, 0, u, t0 : t0 + nt, c0 : c0 + n]

        def like(unit, bank):
            return bank[:].rearrange("p (t b) -> p t b", t=unit[2])

        def sig(u, j):
            h, t = divmod(j, 4)
            v = lg[:, 0, u, t, 512 * h : 512 * h + 512]
            nc.scalar.activation(out=v, in_=v, func=ACT.Sigmoid, scale=2.0, bias=bl[:, 4 * u + t : 4 * u + t + 1])

        def b_mm_d(unit):
            u, t0, nt, c0, n = unit
            db = psum.tile([P, 512], F32, name="dbank", tag="d", bufs=3)
            for t in range(nt):
                mm(db[:, t * n : t * n + n], csq, css, 1, u, t0 + t, c0, c0 + n, True, False)
                mm(db[:, t * n : t * n + n], csq, css, 0, u, t0 + t, c0, c0 + n, False, True)
            st["d", unit] = db

        def b_mm_q(unit):
            u, t0, nt, c0, n = unit
            qb = psum.tile([P, 512], F32, name="qbank", tag="q", bufs=2)
            for t in range(nt):
                mm(qb[:, t * n : t * n + n], csq, css, 0, u, t0 + t, c0, c0 + n, True, True)
            st["q", unit] = qb

        def b_td(unit):
            nc.vector.tensor_tensor(out=zone(unit), in0=like(unit, st["d", unit]), in1=zone(unit), op=ALU.mult)

        def b_qh(unit, flux="S"):
            if flux == "G":
                nc.vector.scalar_tensor_tensor(out=zone(unit), in0=zone(unit), scalar=1.0, in1=like(unit, st["q", unit]), op0=ALU.add, op1=ALU.subtract)
                return
            nc.vector.tensor_tensor(out=zone(unit), in0=zone(unit), in1=like(unit, st["q", unit]), op=ALU.subtract)

        def b_flux(unit, eng):
            v = zone(unit)
            if eng == "V":
                nc.vector.scalar_tensor_tensor(out=v, in0=v, scalar=2.0, in1=v, op0=ALU.add, op1=ALU.mult)
            elif eng == "G":
                nc.gpsimd.tensor_tensor(out=v, in0=v, in1=v, op=ALU.mult)
            else:
                nc.scalar.activation(out=v, in_=v, func=ACT.Square, bias=1.0)

        def b_fin(unit, eng):
            u, t0, nt, c0, n = unit
            if t0 == 0:
                st["pt", u, c0] = work.tile([P, 4, n], BF16, name="pgt", tag="pgt" + str(n), bufs=2)
            dst = st["pt", u, c0]
            for t in range(t0, t0 + nt):
                src = lg[:, 0, u, t, c0 : c0 + n]
                if eng == "V":
                    nc.vector.tensor_scalar(out=dst[:, t, :], in0=src, scalar1=gh[:, u, t : t + 1], scalar2=None, op0=ALU.mult)
                elif eng in "SG":
                    nc.vector.tensor_scalar(out=dst[:, t, :], in0=src, scalar1=gh[:, u, t : t + 1], scalar2=ghn[:, u, t : t + 1], op0=ALU.mult, op1=ALU.add)
                else:
                    nc.scalar.activation(out=dst[:, t, :], in_=src, func=ACT.Identity, scale=gh[:, u, t : t + 1], bias=ghn[:, u, t : t + 1])

        def b_il(u, c0, n):
            nc.vector.tensor_copy(
                out=pg[:, u, 4 * c0 : 4 * (c0 + n)].rearrange("p (c i t) -> p c t i", i=4, t=4),
                in_=st["pt", u, c0][:].rearrange("p t (c i) -> p c t i", i=4))

        def b_quant(u, c0, n):
            nc.vector.quantize_mx(out=pq[:, u, c0 : c0 + n].bitcast(FP8X4), scales=ps8[:, u, c0 : c0 + n], in_=pg[:, u, 4 * c0 : 4 * (c0 + n)])

        def b_out(i):
            ob = psum.tile([P, 512], F32, name="obank", tag="s", bufs=3)
            for u in range(2):
                nc.tensor.matmul_mx(
                    out=ob[:], lhsT=pq[:, u, 128 * i : 128 * i + 128].bitcast(FP8X4), lhsT_scale=ps8[:, u, 128 * i : 128 * i + 128],
                    rhs=dvw[:, u, :].bitcast(FP4X4), rhs_scale=dvs[:, u, :], start=(u == 0), stop=(u == 1))
            st["o", i] = ob

        def b_evac(i, eng):
            ot = work.tile([P, 512], F32, name="ot", tag="ot", bufs=8)
            if eng == "S":
                nc.scalar.copy(out=ot[:], in_=st["o", i][:])
            else:
                nc.vector.tensor_copy(out=ot[:], in_=st["o", i][:])
            nc.sync.dma_start(out=ov[:, i, :], in_=ot[:])


        FLUX0 = "VVVVVVVV"
        FLUX1 = "IIIIISSSS"
        SUB0 = "VVVV"
        SUB1 = "VVVV"
        EVACS = "SSSSSSSS"
        VSQ = ()

        def square(u, t, k, h):
            onv = (u, t, k, h) in VSQ
            a_sq(u, t, k, h, "V" if onv else "S")
            if onv:
                a_mul(u, t, k, h)

        for t in range(4):
            widen(0, 0, "SVVV"[t], (t,))
        turn_x(0, "S")
        ss_il(0, 0, (0,))
        turn_x(1, "S")
        ss_q(0, 0, (0,))
        ss_il(0, 0, (1,))
        quant_x(0, 4)
        ss_q(0, 0, (1,))
        for t in range(4):
            widen(1, 0, "SVVV"[t], (t,))
        for t in range(2):
            square(0, t, 0, 0)
        turn_x(2, "S")
        turn_x(3, "S")
        for t in range(2, 4):
            square(0, t, 0, 0)
        ss_il(1, 0)
        quant_x(4, 8)
        ss_q(1, 0)
        for t in range(4):
            square(0, t, 0, 1)
        for t in range(4):
            square(0, t, 1, 0)
            square(0, t, 1, 1)
        for t in range(4):
            for k in range(2):
                a_ln(0, t, k)
        widen(0, 1, "V")
        ss_il(0, 1)
        widen(1, 1, "V")
        ss_q(0, 1)
        ss_il(1, 1)
        cs_il(0, 0)
        ss_q(1, 1)
        cs_il(1, 0)
        cs_q(0, 0)
        cs_il(0, 1)
        cs_q(1, 0)
        cs_q(0, 1)
        consts()
        for t in range(4):
            a_sub(0, t, SUB0[t])

        def make_units(u, groups):
            res, c0 = [], 0
            for n in groups:
                nt = 512 // n
                res += [(u, t0, nt, c0, n) for t0 in range(0, 4, nt)]
                c0 += n
            return res

        def last_of(unit):
            return unit[1] + unit[2] == 4

        units0 = make_units(0, (512, 512))
        units1 = make_units(1, (256, 256, 256, 128, 128))
        for j in range(8):
            sig(0, j)
        b_mm_d(units0[0])
        b_mm_q(units0[0])
        b_mm_d(units0[1])
        extra = [
            lambda: cs_il(1, 1),
            lambda: cs_q(1, 1),
        ]
        for m in range(TILES + 4):
            n = m - 2
            if 0 <= n < TILES:
                for h in range(2):
                    square(1, n // 2, n % 2, h)
            if 1 <= n < TILES + 1:
                a_ln(1, (n - 1) // 2, (n - 1) % 2)
            if m < TILES:
                b_td(units0[m])
            if m + 2 < TILES:
                b_mm_d(units0[m + 2])
            if 0 <= m - 1 < TILES:
                b_qh(units0[m - 1], FLUX0[m - 1])
            if m + 1 < TILES:
                b_mm_q(units0[m + 1])
            if 0 <= m - 2 < TILES:
                b_flux(units0[m - 2], FLUX0[m - 2])
            if 0 <= m - 3 < TILES:
                b_fin(units0[m - 3], FLUX0[m - 3])
            if 3 <= m < 3 + 2:
                extra[m - 3]()
            if m in (7, 11):
                b_il(0, 512 * (m // 11), 512)
            if m == 8:
                b_quant(0, 0, 512)
            if m >= 6 and m % 2 == 6 % 2 and (m - 6) // 2 < 3:
                a_sub(1, (m - 6) // 2, SUB1[(m - 6) // 2])
        for t in range(4):
            if 2 * t + 6 >= TILES + 4 or t == 3:
                a_sub(1, t, SUB1[t])
        for j in range(5):
            sig(1, j)
        b_mm_d(units1[0])
        b_mm_q(units1[0])
        b_mm_d(units1[1])
        b_quant(0, 512, 512)
        outs = []
        total = len(units1)
        for m in range(total + 5):
            if m < total:
                b_td(units1[m])
            if m + 2 < total:
                b_mm_d(units1[m + 2])
            if 0 <= m - 1 < total:
                b_qh(units1[m - 1], FLUX1[m - 1])
            if m + 1 < total:
                b_mm_q(units1[m + 1])
            if 0 <= m - 2 < total:
                b_flux(units1[m - 2], FLUX1[m - 2])
            if m + 5 < 8:
                sig(1, m + 5)
            for _ in range(1):
                if outs and outs[0][0] <= m - 2:
                    i = outs.pop(0)[1]
                    b_evac(i, EVACS[i])
            done = units1[m - 4] if 0 <= m - 4 < total and last_of(units1[m - 4]) else None
            if done:
                b_il(1, done[3], done[4])
            if 0 <= m - 3 < total:
                b_fin(units1[m - 3], FLUX1[m - 3])
            if done:
                b_quant(1, done[3], done[4])
                for i in range(done[3] // 128, (done[3] + done[4]) // 128):
                    b_out(i)
                    outs.append((m, i))
        for m, i in outs:
            b_evac(i, EVACS[i])
